import numpy as np
import ml_dtypes


def mxq(x, axis, fmt="e4m3"):
    dtype, down = {"e4m3": (ml_dtypes.float8_e4m3fn, 7), "e5m2": (ml_dtypes.float8_e5m2, 14)}[fmt]
    v = np.moveaxis(np.asarray(x, np.float32).astype(ml_dtypes.bfloat16).astype(np.float64), axis, -1)
    blocks = v.reshape(v.shape[:-1] + (-1, 32))
    amax = np.abs(blocks).max(-1, keepdims=True)
    byte = np.maximum(np.where(amax > 0, np.frexp(amax)[1] - 1 + 127, 0) - down, 1)
    scale = np.exp2(byte - 127.0)
    codes = (blocks / scale).astype(np.float32).astype(dtype).astype(np.float64)
    return np.moveaxis((codes * scale).reshape(v.shape), -1, axis)


WIDE = False


def mx_kscale(k):
    if not WIDE:
        return np.ones(k)
    levels = np.array([10, -10, 5, -5, 0])
    if k % 512:
        return np.exp2(np.random.permutation(np.resize(levels, k // 32))).repeat(32)
    a = np.empty((k // 512, 16))
    for p in range(k // 512):
        a[p, :8] = np.random.permutation(np.resize(levels, 8))
        for g in range(8):
            far = levels[np.abs(levels - a[p, g]) >= 10]
            a[p, g + 8] = far[np.random.randint(len(far))]
    return np.exp2(a.ravel()).repeat(32)


def f64(x):
    return np.asarray(x).astype(np.float64)


def striped(idx):
    return np.tile(idx.reshape(-1, 16).T, (8, 1)).astype(np.uint16)


def unstriped(offs):
    return offs[:16].T.reshape(-1).astype(np.int64)


E2M1 = np.array([0.0, 0.5, 1.0, 1.5, 2.0, 3.0, 4.0, 6.0, -0.0, -0.5, -1.0, -1.5, -2.0, -3.0, -4.0, -6.0])


def pack_weight(w, fmt):
    k, n = w.shape
    w = f64(np.asarray(w, np.float32).astype(ml_dtypes.bfloat16)).reshape(k // 32, 32, n)
    amax = np.abs(w).max(1)
    if fmt == "e4m3":
        byte = np.frexp(amax)[1] - 1 + 127 - 7
    else:
        mant, ex = np.frexp(amax / 6.0)
        byte = np.where(mant > 0.5, ex, ex - 1) + 127
    byte = np.clip(np.where(amax > 0, byte, 1), 1, 254)
    scaled = (w * np.exp2(127.0 - byte)[:, None, :]).reshape(k, n).astype(np.float32)
    by_word = np.ascontiguousarray(scaled.reshape(k // 512, 128, 4, n).transpose(0, 1, 3, 2))
    if fmt == "e4m3":
        words = by_word.astype(ml_dtypes.float8_e4m3fn).view(np.uint8)
    else:
        c = by_word.astype(ml_dtypes.float4_e2m1fn).view(np.uint8) & 0xF
        words = (c[..., 0::2] | (c[..., 1::2] << 4)).reshape(k // 512, 128, 2 * n)
    return np.ascontiguousarray(words), np.ascontiguousarray(byte.astype(np.uint8).reshape(k // 512, 16, n))


def unpack_weight(words, scales, fmt):
    g, _, n = scales.shape
    words = np.ascontiguousarray(words).reshape(g, 128, n, -1)
    if fmt == "e4m3":
        vals = words.view(ml_dtypes.float8_e4m3fn).astype(np.float64)
    else:
        nib = np.empty((g, 128, n, 4), np.uint8)
        nib[..., 0::2] = words & 0xF
        nib[..., 1::2] = words >> 4
        vals = E2M1[nib]
    vals = vals * np.repeat(np.exp2(scales.astype(np.float64) - 127.0), 8, axis=1)[..., None]
    return vals.transpose(0, 1, 3, 2).reshape(g * 512, n)


def silu(v):
    return v / (1.0 + np.exp(-np.maximum(v, -700.0)))


K, T, E, C, H, N = 512, 1024, 16, 128, 512, 128


def by_expert(wq, xq):
    return np.concatenate([wq[e].T @ xq[:, e * C:(e + 1) * C] for e in range(E)], axis=1)


def setup_inputs():
    n = np.random.standard_normal
    s = mx_kscale(K)[:, None]
    u = mx_kscale(H)
    first = np.random.permutation(np.repeat(np.arange(E), T // E))
    second = (first + 1 + np.random.permutation(np.repeat(np.arange(E - 1), -(-T // (E - 1)))[:T])) % E
    while np.bincount(second, minlength=E).max() != T // E:
        load = np.bincount(second, minlength=E); hi, lo = int(load.argmax()), int(load.argmin())
        t = np.flatnonzero((second == hi) & (first != lo))[0]; second[t] = lo
    slot_token = np.empty(E * C, np.int64); pos = np.empty((2, T), np.int64); fill = np.zeros(E, np.int64)
    place = np.stack([np.random.permutation(C) for _ in range(E)])
    for r, deal in enumerate((first, second)):
        for t in np.random.permutation(T):
            e = deal[t]; j = e * C + place[e, fill[e]]; fill[e] += 1; slot_token[j] = t; pos[r, t] = j
    g = np.random.uniform(0.2, 0.8, T)
    w1 = [pack_weight(m, "e2m1") for m in n((E, K, H)) / np.sqrt(K) / s[None] * u[None, None, :]]
    w2 = [pack_weight(m, "e2m1") for m in n((E, H, N)) / np.sqrt(H) / u[None, :, None]]
    return {
        "xT": (n((K, T)) * s).astype(np.float32),
        "w1_words": np.stack([m[0] for m in w1]),
        "w1_scales": np.stack([m[1] for m in w1]),
        "w2_words": np.stack([m[0] for m in w2]),
        "w2_scales": np.stack([m[1] for m in w2]),
        "gate": np.stack([np.tile(g, (N, 1)), np.tile(1.0 - g, (N, 1))]).astype(np.float32),
        "offs": striped(slot_token),
        "pos1": striped(pos[0]),
        "pos2": striped(pos[1]),
    }


def reference(xT, w1_words, w1_scales, w2_words, w2_scales, gate, offs, pos1, pos2):
    idx = unstriped(offs)
    w1 = np.stack([unpack_weight(w1_words[e], w1_scales[e], "e2m1") for e in range(E)])
    w2 = np.stack([unpack_weight(w2_words[e], w2_scales[e], "e2m1") for e in range(E)])
    xq = mxq(f64(xT)[:, idx], 0, "e4m3")
    h = silu(by_expert(w1, xq))
    y = by_expert(w2, mxq(h, 0, "e4m3"))
    return f64(gate[0]) * y[:, unstriped(pos1)] + f64(gate[1]) * y[:, unstriped(pos2)]

@@ -1,0 +1,222 @@
+from contextlib import ExitStack
+
+import concourse.mybir as mybir
+from concourse.masks import make_identity
+
+K, T, E, C, H, N = 512, 1024, 16, 128, 512, 128
+S = E * C
+P = 128
+FLOPS = 2 * K * H * S + 2 * H * N * S
+
+F32 = mybir.dt.float32
+BF16 = mybir.dt.bfloat16
+I32 = mybir.dt.int32
+U32 = mybir.dt.uint32
+U16 = mybir.dt.uint16
+U8 = mybir.dt.uint8
+FP8X4 = mybir.dt.float8_e4m3fn_x4
+FP4X4 = mybir.dt.float4_e2m1fn_x4
+SILU = mybir.ActivationFunctionType.Silu
+MULT = mybir.AluOpType.mult
+ADD = mybir.AluOpType.add
+
+XC = 256
+XV = 160
+UNIT = 2
+
+
+def tile_moe_pln_mlp_silu_kernel(
+    tc, xT, w1_words, w1_scales, w2_words, w2_scales, gate, offs, pos1, pos2, out
+):
+    nc = tc.nc
+    with ExitStack() as ctx:
+        lists = ctx.enter_context(tc.tile_pool(name="lists", bufs=1))
+        keep = ctx.enter_context(tc.tile_pool(name="keep", bufs=1))
+        ring = ctx.enter_context(tc.tile_pool(name="ring", bufs=3))
+        psum = ctx.enter_context(tc.psum_pool(name="psum", bufs=2))
+
+        offs_sb = lists.tile([P, S // 16], U16, name="offs_sb")
+        pos1_sb = lists.tile([P, T // 16], U16, name="pos1_sb")
+        pos2_sb = lists.tile([P, T // 16], U16, name="pos2_sb")
+
+        x_words = keep.tile([P, T], U32, name="x_words", align_bytes=64)
+        x_scales = keep.tile([P, T], U8, name="x_scales", align_bytes=64)
+        g_words = keep.tile([P, S], U32, name="g_words", align_bytes=64)
+        g_scales = keep.tile([P, S], U8, name="g_scales", align_bytes=64)
+        w1_sb = keep.tile([P, E, 2 * H], U8, name="w1_sb", align_bytes=64)
+        w1s_sb = keep.tile([P, E, H], U8, name="w1s_sb", align_bytes=64)
+        w2_sb = keep.tile([P, E, 2 * N], U8, name="w2_sb", align_bytes=64)
+        w2s_sb = keep.tile([P, E, N], U8, name="w2s_sb", align_bytes=64)
+        gate_sb = keep.tile([P, 2, T], F32, name="gate_sb")
+        y_sb = keep.tile([P, S], F32, name="y_sb")
+        ident = keep.tile([P, P], F32, name="ident")
+        warm = keep.tile([P, 1], F32, name="warm")
+
+        nc.sync.dma_start(offs_sb[:], offs)
+        raws = []
+        for c in range(T // XC):
+            raw = keep.tile([P, 4, XC], F32, name=f"raw{c}")
+            nc.sync.dma_start(out=raw[:], in_=xT[:, c * XC : (c + 1) * XC].rearrange("(p j) w -> p j w", j=4))
+            raws.append(raw)
+
+        nc.gpsimd.memset(x_scales[:], 0)
+        nc.vector.memset(w1s_sb[:].rearrange("p e i -> p (e i)").bitcast(I32), 0)
+        nc.vector.memset(w2s_sb[:].rearrange("p e i -> p (e i)").bitcast(I32), 0)
+        nc.vector.memset(warm[:], 0.0)
+        nc.scalar.activation(warm[:], warm[:], SILU)
+        make_identity(nc, ident[:])
+
+        def load_w1s(e0, e1):
+            for q in range(4):
+                nc.sync.dma_start(
+                    out=w1s_sb[32 * q : 32 * q + 4, e0:e1, :].bitcast(I32),
+                    in_=w1_scales[e0:e1, 0, 4 * q : 4 * q + 4, :].rearrange("e r i -> r e i").bitcast(I32),
+                )
+
+        load_w1s(0, 4)
+
+        def load_w1(e0, e1):
+            nc.sync.dma_start(
+                out=w1_sb[:, e0:e1, :].bitcast(I32),
+                in_=w1_words[e0:e1, 0].rearrange("e p b -> p e b").bitcast(I32),
+            )
+
+        def load_w2(e0, e1):
+            nc.sync.dma_start(
+                out=w2_sb[:, e0:e1, :].bitcast(I32),
+                in_=w2_words[e0:e1, 0].rearrange("e p b -> p e b").bitcast(I32),
+            )
+
+        load_w1(0, 2)
+        load_w1s(4, 16)
+        for q in range(4):
+            nc.sync.dma_start(
+                out=w2s_sb[32 * q : 32 * q + 4, :, :].bitcast(I32),
+                in_=w2_scales[:, 0, 4 * q : 4 * q + 4, :].rearrange("e r i -> r e i").bitcast(I32),
+            )
+        load_w1(2, 4)
+        load_w2(0, 8)
+        load_w1(4, 8)
+        load_w2(8, 16)
+        load_w1(8, 12)
+        load_w1(12, 16)
+        nc.sync.dma_start(pos1_sb[:], pos1)
+        nc.sync.dma_start(pos2_sb[:], pos2)
+        nc.sync.dma_start(out=gate_sb[:, 0, :], in_=gate[0])
+        nc.sync.dma_start(out=gate_sb[:, 1, :], in_=gate[1])
+
+        for c in range(T // XC):
+            grouped = ring.tile([P, XC, 4], BF16, name="grouped", align_bytes=64)
+            src = raws[c][:].rearrange("p j w -> p w j")
+            nc.vector.tensor_copy(out=grouped[:, :XV, :], in_=src[:, :XV, :])
+            nc.scalar.copy(out=grouped[:, XV:, :], in_=src[:, XV:, :])
+            nc.vector.quantize_mx(
+                out=x_words[:, c * XC : (c + 1) * XC].bitcast(FP8X4),
+                scales=x_scales[:, c * XC : (c + 1) * XC],
+                in_=grouped[:].rearrange("p w j -> p (w j)"),
+            )
+
+        US = UNIT * C
+        state = {}
+
+        def gather(e0, e1):
+            cols = slice(e0 * C, e1 * C)
+            lst = offs_sb[:, e0 * C // 16 : e1 * C // 16]
+            nc.vector.tensor_copy(out=g_words[:, cols], in_=x_words[:].indirect(lst))
+            nc.vector.tensor_copy(out=g_scales[:, cols], in_=x_scales[:].indirect(lst))
+
+        def first(u):
+            h_tiles = []
+            for i in range(UNIT):
+                e = u * UNIT + i
+                cols = slice(e * C, (e + 1) * C)
+                a_ps = psum.tile([P, H], F32, name="a_ps", bufs=4)
+                nc.tensor.matmul_mx(
+                    out=a_ps[:],
+                    lhsT=g_words[:, cols].bitcast(FP8X4),
+                    lhsT_scale=g_scales[:, cols],
+                    rhs=w1_sb[:, e, :].bitcast(FP4X4),
+                    rhs_scale=w1s_sb[:, e, :],
+                    start=True,
+                    stop=True,
+                )
+                h_sb = ring.tile([P, 2, P, 2], BF16, name="h_sb", bufs=6, align_bytes=64)
+                nc.scalar.activation(h_sb[:], a_ps[:].rearrange("s (p u d) -> s u p d", u=2, d=2), SILU)
+                h_tiles.append(h_sb)
+            state[u] = h_tiles
+
+        def second(u):
+            t_ps = psum.tile([P, 2, US], F32, name="t_ps", bufs=2)
+            for i in range(UNIT):
+                words = state[u][i][:].rearrange("s u p d -> s (u p d)").bitcast(F32)
+                for v in range(2):
+                    nc.tensor.transpose(t_ps[:, v, i * C : (i + 1) * C], words[:, v * P : (v + 1) * P], ident[:])
+            hg = ring.tile([P, US, 4], BF16, name="hg", align_bytes=64)
+            hg_words = hg[:].rearrange("p s j -> p (s j)").bitcast(F32).rearrange("p (s v) -> p s v", v=2)
+            if u % 3 == 2:
+                nc.vector.tensor_copy(out=hg_words, in_=t_ps[:].rearrange("p v s -> p s v"))
+            else:
+                nc.scalar.copy(out=hg_words, in_=t_ps[:].rearrange("p v s -> p s v"))
+            state[u] = hg
+
+        banks = {}
+
+        def third(u):
+            hg = state[u]
+            h_words = ring.tile([P, US], U32, name="h_words", align_bytes=64)
+            h_scales = ring.tile([P, US], U8, name="h_scales", align_bytes=64)
+            nc.vector.quantize_mx(
+                out=h_words[:].bitcast(FP8X4), scales=h_scales[:], in_=hg[:].rearrange("p s j -> p (s j)")
+            )
+            wide = 2 if u < 6 else 1
+            if u % wide == 0:
+                y_ps = psum.tile([P, wide * US], F32, name="y_ps", bufs=2)
+                banks[0] = y_ps
+            y_ps = banks[0]
+            for i in range(UNIT):
+                e = u * UNIT + i
+                k = (u % wide) * UNIT + i
+                cols = slice(i * C, (i + 1) * C)
+                nc.tensor.matmul_mx(
+                    out=y_ps[:, k * C : (k + 1) * C],
+                    lhsT=w2_sb[:, e, :].bitcast(FP4X4),
+                    lhsT_scale=w2s_sb[:, e, :],
+                    rhs=h_words[:, cols].bitcast(FP8X4),
+                    rhs_scale=h_scales[:, cols],
+                    start=True,
+                    stop=True,
+                )
+            if u % wide == wide - 1:
+                cols = slice((u + 1 - wide) * US, (u + 1) * US)
+                if u == 6:
+                    nc.scalar.copy(out=y_sb[:, cols], in_=y_ps[:])
+                else:
+                    nc.vector.tensor_copy(out=y_sb[:, cols], in_=y_ps[:])
+
+        units = E // UNIT
+        groups = [1, 1, 2, 4, 4, 4]
+        have = 0
+        for u in range(units):
+            while groups and have < UNIT * (u + 2):
+                n = groups.pop(0)
+                gather(have, have + n)
+                have += n
+            first(u)
+            if u >= 1:
+                second(u - 1)
+                third(u - 1)
+        second(units - 1)
+        third(units - 1)
+
+        t0 = 0
+        for w in (512, 256, 256):
+            cols = slice(t0, t0 + w)
+            rows = slice(t0 // 16, (t0 + w) // 16)
+            o1 = ring.tile([P, w], F32, name=f"o1_{w}")
+            o2 = ring.tile([P, w], F32, name=f"o2_{w}")
+            nc.vector.tensor_tensor(o1[:], y_sb[:].indirect(pos1_sb[:, rows]), gate_sb[:, 0, cols], MULT)
+            nc.vector.tensor_tensor(o2[:], y_sb[:].indirect(pos2_sb[:, rows]), gate_sb[:, 1, cols], MULT)
+            o = ring.tile([P, w], F32, name=f"o_{w}")
+            nc.vector.tensor_tensor(o[:], o1[:], o2[:], ADD)
+            nc.sync.dma_start(out=out[:, cols], in_=o[:])
+            t0 += w

@@ -20,9 +20,15 @@ SILU = mybir.ActivationFunctionType.Silu
 MULT = mybir.AluOpType.mult
 ADD = mybir.AluOpType.add
 
-XC = 256
-XV = 160
-UNIT = 2
+X_CHUNKS = [256,256,256,256]
+X_VECTOR = [160,160,160,160]
+UNITS = [1,1,2,2,2,2,2,2,1,1]
+GROUPS = [1,1,2,2,2,2,2,2,2]
+T_ENG = "SSSSSSSSSS"
+Y_ENG = "VVVSVVSVSV"
+LT, LQ, LY, LEAD = 2, 3, 4, 2
+PERM = "GFSQY"
+TAIL = [512,384,128]
 
 
 def tile_moe_pln_mlp_silu_kernel(
@@ -41,8 +47,6 @@ def tile_moe_pln_mlp_silu_kernel(
 
         x_words = keep.tile([P, T], U32, name="x_words", align_bytes=64)
         x_scales = keep.tile([P, T], U8, name="x_scales", align_bytes=64)
-        g_words = keep.tile([P, S], U32, name="g_words", align_bytes=64)
-        g_scales = keep.tile([P, S], U8, name="g_scales", align_bytes=64)
         w1_sb = keep.tile([P, E, 2 * H], U8, name="w1_sb", align_bytes=64)
         w1s_sb = keep.tile([P, E, H], U8, name="w1s_sb", align_bytes=64)
         w2_sb = keep.tile([P, E, 2 * N], U8, name="w2_sb", align_bytes=64)
@@ -54,16 +58,18 @@ def tile_moe_pln_mlp_silu_kernel(
 
         nc.sync.dma_start(offs_sb[:], offs)
         raws = []
-        for c in range(T // XC):
-            raw = keep.tile([P, 4, XC], F32, name=f"raw{c}")
-            nc.sync.dma_start(out=raw[:], in_=xT[:, c * XC : (c + 1) * XC].rearrange("(p j) w -> p j w", j=4))
+        t0 = 0
+        for c, w in enumerate(X_CHUNKS):
+            raw = keep.tile([P, 4, w], F32, name=f"raw{c}")
+            nc.sync.dma_start(out=raw[:], in_=xT[:, t0 : t0 + w].rearrange("(p j) w -> p j w", j=4))
             raws.append(raw)
+            t0 += w
 
+        nc.vector.memset(warm[:], 0.0)
+        nc.scalar.activation(warm[:], warm[:], SILU)
         nc.gpsimd.memset(x_scales[:], 0)
         nc.vector.memset(w1s_sb[:].rearrange("p e i -> p (e i)").bitcast(I32), 0)
         nc.vector.memset(w2s_sb[:].rearrange("p e i -> p (e i)").bitcast(I32), 0)
-        nc.vector.memset(warm[:], 0.0)
-        nc.scalar.activation(warm[:], warm[:], SILU)
         make_identity(nc, ident[:])
 
         def load_w1s(e0, e1):
@@ -73,7 +79,12 @@ def tile_moe_pln_mlp_silu_kernel(
                     in_=w1_scales[e0:e1, 0, 4 * q : 4 * q + 4, :].rearrange("e r i -> r e i").bitcast(I32),
                 )
 
-        load_w1s(0, 4)
+        def load_w2s(e0, e1):
+            for q in range(4):
+                nc.sync.dma_start(
+                    out=w2s_sb[32 * q : 32 * q + 4, e0:e1, :].bitcast(I32),
+                    in_=w2_scales[e0:e1, 0, 4 * q : 4 * q + 4, :].rearrange("e r i -> r e i").bitcast(I32),
+                )
 
         def load_w1(e0, e1):
             nc.sync.dma_start(
@@ -87,98 +98,104 @@ def tile_moe_pln_mlp_silu_kernel(
                 in_=w2_words[e0:e1, 0].rearrange("e p b -> p e b").bitcast(I32),
             )
 
+        load_w1s(0, 4)
         load_w1(0, 2)
         load_w1s(4, 16)
-        for q in range(4):
-            nc.sync.dma_start(
-                out=w2s_sb[32 * q : 32 * q + 4, :, :].bitcast(I32),
-                in_=w2_scales[:, 0, 4 * q : 4 * q + 4, :].rearrange("e r i -> r e i").bitcast(I32),
-            )
+        load_w2s(0, 16)
         load_w1(2, 4)
-        load_w2(0, 8)
+        load_w2(0, 4)
         load_w1(4, 8)
-        load_w2(8, 16)
+        load_w2(4, 8)
         load_w1(8, 12)
+        load_w2(8, 16)
         load_w1(12, 16)
         nc.sync.dma_start(pos1_sb[:], pos1)
         nc.sync.dma_start(pos2_sb[:], pos2)
         nc.sync.dma_start(out=gate_sb[:, 0, :], in_=gate[0])
         nc.sync.dma_start(out=gate_sb[:, 1, :], in_=gate[1])
 
-        for c in range(T // XC):
-            grouped = ring.tile([P, XC, 4], BF16, name="grouped", align_bytes=64)
+        t0 = 0
+        for c, w in enumerate(X_CHUNKS):
+            grouped = ring.tile([P, w, 4], BF16, name="grouped", align_bytes=64)
             src = raws[c][:].rearrange("p j w -> p w j")
-            nc.vector.tensor_copy(out=grouped[:, :XV, :], in_=src[:, :XV, :])
-            nc.scalar.copy(out=grouped[:, XV:, :], in_=src[:, XV:, :])
+            v = X_VECTOR[c]
+            if v > 0:
+                nc.vector.tensor_copy(out=grouped[:, :v, :], in_=src[:, :v, :])
+            if v < w:
+                nc.scalar.copy(out=grouped[:, v:, :], in_=src[:, v:, :])
             nc.vector.quantize_mx(
-                out=x_words[:, c * XC : (c + 1) * XC].bitcast(FP8X4),
-                scales=x_scales[:, c * XC : (c + 1) * XC],
+                out=x_words[:, t0 : t0 + w].bitcast(FP8X4),
+                scales=x_scales[:, t0 : t0 + w],
                 in_=grouped[:].rearrange("p w j -> p (w j)"),
             )
+            t0 += w
 
-        US = UNIT * C
-        state = {}
+        starts = [sum(UNITS[:u]) for u in range(len(UNITS))]
+        g_tiles, h_tiles, hg_tiles, q_tiles = {}, {}, {}, {}
 
         def gather(e0, e1):
-            cols = slice(e0 * C, e1 * C)
+            w = (e1 - e0) * C
             lst = offs_sb[:, e0 * C // 16 : e1 * C // 16]
-            nc.vector.tensor_copy(out=g_words[:, cols], in_=x_words[:].indirect(lst))
-            nc.vector.tensor_copy(out=g_scales[:, cols], in_=x_scales[:].indirect(lst))
+            g_words = ring.tile([P, w], U32, name="g_words", bufs=3, align_bytes=64)
+            g_scales = ring.tile([P, w], U8, name="g_scales", bufs=3, align_bytes=64)
+            nc.vector.tensor_copy(out=g_words[:], in_=x_words[:].indirect(lst))
+            nc.vector.tensor_copy(out=g_scales[:], in_=x_scales[:].indirect(lst))
+            for e in range(e0, e1):
+                slots = slice((e - e0) * C, (e - e0 + 1) * C)
+                g_tiles[e] = g_words[:, slots], g_scales[:, slots]
 
         def first(u):
-            h_tiles = []
-            for i in range(UNIT):
-                e = u * UNIT + i
-                cols = slice(e * C, (e + 1) * C)
+            h_tiles[u] = []
+            for i in range(UNITS[u]):
+                e = starts[u] + i
+                words, scales = g_tiles[e]
                 a_ps = psum.tile([P, H], F32, name="a_ps", bufs=4)
                 nc.tensor.matmul_mx(
                     out=a_ps[:],
-                    lhsT=g_words[:, cols].bitcast(FP8X4),
-                    lhsT_scale=g_scales[:, cols],
+                    lhsT=words.bitcast(FP8X4),
+                    lhsT_scale=scales,
                     rhs=w1_sb[:, e, :].bitcast(FP4X4),
                     rhs_scale=w1s_sb[:, e, :],
                     start=True,
                     stop=True,
                 )
-                h_sb = ring.tile([P, 2, P, 2], BF16, name="h_sb", bufs=6, align_bytes=64)
+                h_sb = ring.tile([P, 2, P, 2], BF16, name="h_sb", bufs=8, align_bytes=64)
                 nc.scalar.activation(h_sb[:], a_ps[:].rearrange("s (p u d) -> s u p d", u=2, d=2), SILU)
-                h_tiles.append(h_sb)
-            state[u] = h_tiles
+                h_tiles[u].append(h_sb)
 
-        def second(u):
-            t_ps = psum.tile([P, 2, US], F32, name="t_ps", bufs=2)
-            for i in range(UNIT):
-                words = state[u][i][:].rearrange("s u p d -> s (u p d)").bitcast(F32)
+        def turn(u):
+            w = UNITS[u] * C
+            t_ps = psum.tile([P, 2, w], F32, name="t_ps", bufs=2)
+            for i in range(UNITS[u]):
+                words = h_tiles[u][i][:].rearrange("s u p d -> s (u p d)").bitcast(F32)
                 for v in range(2):
                     nc.tensor.transpose(t_ps[:, v, i * C : (i + 1) * C], words[:, v * P : (v + 1) * P], ident[:])
-            hg = ring.tile([P, US, 4], BF16, name="hg", align_bytes=64)
+            hg = ring.tile([P, w, 4], BF16, name="hg", align_bytes=64)
             hg_words = hg[:].rearrange("p s j -> p (s j)").bitcast(F32).rearrange("p (s v) -> p s v", v=2)
-            if u % 3 == 2:
+            if T_ENG[u] == "V":
                 nc.vector.tensor_copy(out=hg_words, in_=t_ps[:].rearrange("p v s -> p s v"))
             else:
                 nc.scalar.copy(out=hg_words, in_=t_ps[:].rearrange("p v s -> p s v"))
-            state[u] = hg
+            hg_tiles[u] = hg
 
-        banks = {}
-
-        def third(u):
-            hg = state[u]
-            h_words = ring.tile([P, US], U32, name="h_words", align_bytes=64)
-            h_scales = ring.tile([P, US], U8, name="h_scales", align_bytes=64)
+        def quantize(u):
+            w = UNITS[u] * C
+            h_words = ring.tile([P, w], U32, name="h_words", align_bytes=64)
+            h_scales = ring.tile([P, w], U8, name="h_scales", align_bytes=64)
             nc.vector.quantize_mx(
-                out=h_words[:].bitcast(FP8X4), scales=h_scales[:], in_=hg[:].rearrange("p s j -> p (s j)")
+                out=h_words[:].bitcast(FP8X4), scales=h_scales[:], in_=hg_tiles[u][:].rearrange("p s j -> p (s j)")
             )
-            wide = 2 if u < 6 else 1
-            if u % wide == 0:
-                y_ps = psum.tile([P, wide * US], F32, name="y_ps", bufs=2)
-                banks[0] = y_ps
-            y_ps = banks[0]
-            for i in range(UNIT):
-                e = u * UNIT + i
-                k = (u % wide) * UNIT + i
+            q_tiles[u] = h_words, h_scales
+
+        def second(u):
+            w = UNITS[u] * C
+            h_words, h_scales = q_tiles[u]
+            y_ps = psum.tile([P, w], F32, name="y_ps", bufs=2)
+            for i in range(UNITS[u]):
+                e = starts[u] + i
                 cols = slice(i * C, (i + 1) * C)
                 nc.tensor.matmul_mx(
-                    out=y_ps[:, k * C : (k + 1) * C],
+                    out=y_ps[:, cols],
                     lhsT=w2_sb[:, e, :].bitcast(FP4X4),
                     lhsT_scale=w2s_sb[:, e, :],
                     rhs=h_words[:, cols].bitcast(FP8X4),
@@ -186,37 +203,51 @@ def tile_moe_pln_mlp_silu_kernel(
                     start=True,
                     stop=True,
                 )
-            if u % wide == wide - 1:
-                cols = slice((u + 1 - wide) * US, (u + 1) * US)
-                if u == 6:
-                    nc.scalar.copy(out=y_sb[:, cols], in_=y_ps[:])
-                else:
-                    nc.vector.tensor_copy(out=y_sb[:, cols], in_=y_ps[:])
+            cols = slice(starts[u] * C, starts[u] * C + w)
+            if Y_ENG[u] == "V":
+                nc.vector.tensor_copy(out=y_sb[:, cols], in_=y_ps[:])
+            else:
+                nc.scalar.copy(out=y_sb[:, cols], in_=y_ps[:])
 
-        units = E // UNIT
-        groups = [1, 1, 2, 4, 4, 4]
+        n = len(UNITS)
+        groups = list(GROUPS)
         have = 0
-        for u in range(units):
-            while groups and have < UNIT * (u + 2):
-                n = groups.pop(0)
-                gather(have, have + n)
-                have += n
-            first(u)
-            if u >= 1:
-                second(u - 1)
-                third(u - 1)
-        second(units - 1)
-        third(units - 1)
+        for s in range(n + LY):
+            for stage in PERM:
+                if stage == "G":
+                    last = min(n - 1, s + LEAD)
+                    while have < starts[last] + UNITS[last]:
+                        gather(have, have + groups[0])
+                        have += groups.pop(0)
+                if stage == "F" and s < n:
+                    first(s)
+                if stage == "S" and 0 <= s - LT < n:
+                    turn(s - LT)
+                if stage == "Q" and 0 <= s - LQ < n:
+                    quantize(s - LQ)
+                if stage == "Y" and 0 <= s - LY < n:
+                    second(s - LY)
 
-        t0 = 0
-        for w in (512, 256, 256):
-            cols = slice(t0, t0 + w)
+        tail_starts = [sum(TAIL[:k]) for k in range(len(TAIL))]
+        halves = {}
+
+        def fetch(k, r):
+            t0, w = tail_starts[k], TAIL[k]
             rows = slice(t0 // 16, (t0 + w) // 16)
-            o1 = ring.tile([P, w], F32, name=f"o1_{w}")
-            o2 = ring.tile([P, w], F32, name=f"o2_{w}")
-            nc.vector.tensor_tensor(o1[:], y_sb[:].indirect(pos1_sb[:, rows]), gate_sb[:, 0, cols], MULT)
-            nc.vector.tensor_tensor(o2[:], y_sb[:].indirect(pos2_sb[:, rows]), gate_sb[:, 1, cols], MULT)
-            o = ring.tile([P, w], F32, name=f"o_{w}")
-            nc.vector.tensor_tensor(o[:], o1[:], o2[:], ADD)
-            nc.sync.dma_start(out=out[:, cols], in_=o[:])
-            t0 += w
+            half = ring.tile([P, w], F32, name=f"half{r}_{k}", bufs=1)
+            pos = (pos1_sb, pos2_sb)[r]
+            nc.vector.tensor_tensor(half[:], y_sb[:].indirect(pos[:, rows]), gate_sb[:, r, t0 : t0 + w], MULT)
+            halves[k, r] = half
+
+        def add(k):
+            t0, w = tail_starts[k], TAIL[k]
+            o = ring.tile([P, w], F32, name=f"o_{k}", bufs=1)
+            nc.vector.tensor_tensor(o[:], halves[k, 0][:], halves[k, 1][:], ADD)
+            nc.sync.dma_start(out=out[:, t0 : t0 + w], in_=o[:])
+
+        for k in range(len(TAIL)):
+            fetch(k, 0)
+            if k > 0:
+                add(k - 1)
+            fetch(k, 1)
+        add(len(TAIL) - 1)

@@ -24,10 +24,10 @@ X_CHUNKS = [256,256,256,256]
 X_VECTOR = [160,160,160,160]
 UNITS = [1,1,2,2,2,2,2,2,1,1]
 GROUPS = [1,1,2,2,2,2,2,2,2]
-T_ENG = "SSSSSSSSSS"
-Y_ENG = "VVVSVVSVSV"
+T_ENG = "SSSSSSSSVV"
+Y_ENG = "VVVVVVVVSS"
 LT, LQ, LY, LEAD = 2, 3, 4, 2
-PERM = "GFSQY"
+PERM = "QYSGF"
 TAIL = [512,384,128]
 
 
@@ -100,15 +100,15 @@ def tile_moe_pln_mlp_silu_kernel(
 
         load_w1s(0, 4)
         load_w1(0, 2)
-        load_w1s(4, 16)
-        load_w2s(0, 16)
         load_w1(2, 4)
-        load_w2(0, 4)
+        load_w1s(4, 16)
         load_w1(4, 8)
-        load_w2(4, 8)
+        load_w2s(0, 16)
+        load_w2(0, 4)
         load_w1(8, 12)
-        load_w2(8, 16)
+        load_w2(4, 8)
         load_w1(12, 16)
+        load_w2(8, 16)
         nc.sync.dma_start(pos1_sb[:], pos1)
         nc.sync.dma_start(pos2_sb[:], pos2)
         nc.sync.dma_start(out=gate_sb[:, 0, :], in_=gate[0])

@@ -22,12 +22,12 @@ ADD = mybir.AluOpType.add
 
 X_CHUNKS = [256,256,256,256]
 X_VECTOR = [160,160,160,160]
-UNITS = [1,1,2,2,2,2,2,2,1,1]
+UNITS = [1,1,2,2,2,2,2,2,2]
 GROUPS = [1,1,2,2,2,2,2,2,2]
-T_ENG = "SSSSSSSSVV"
-Y_ENG = "VVVVVVVVSS"
+T_ENG = "SSSSSSSSS"
+Y_ENG = "VVVVVVVVV"
 LT, LQ, LY, LEAD = 2, 3, 4, 2
-PERM = "QYSGF"
+PERM = "SQYGF"
 TAIL = [512,384,128]
 
 
@@ -228,26 +228,26 @@ def tile_moe_pln_mlp_silu_kernel(
                 if stage == "Y" and 0 <= s - LY < n:
                     second(s - LY)
 
+        first_half = keep.tile([P, T], F32, name="first_half")
+        nc.vector.tensor_tensor(first_half[:], y_sb[:].indirect(pos1_sb[:]), gate_sb[:, 0, :], MULT)
         tail_starts = [sum(TAIL[:k]) for k in range(len(TAIL))]
-        halves = {}
+        second_half = {}
 
-        def fetch(k, r):
+        def fetch(k):
             t0, w = tail_starts[k], TAIL[k]
+            half = ring.tile([P, w], F32, name=f"half_{k}", bufs=1)
             rows = slice(t0 // 16, (t0 + w) // 16)
-            half = ring.tile([P, w], F32, name=f"half{r}_{k}", bufs=1)
-            pos = (pos1_sb, pos2_sb)[r]
-            nc.vector.tensor_tensor(half[:], y_sb[:].indirect(pos[:, rows]), gate_sb[:, r, t0 : t0 + w], MULT)
-            halves[k, r] = half
+            nc.vector.tensor_tensor(half[:], y_sb[:].indirect(pos2_sb[:, rows]), gate_sb[:, 1, t0 : t0 + w], MULT)
+            second_half[k] = half
 
         def add(k):
             t0, w = tail_starts[k], TAIL[k]
             o = ring.tile([P, w], F32, name=f"o_{k}", bufs=1)
-            nc.vector.tensor_tensor(o[:], halves[k, 0][:], halves[k, 1][:], ADD)
+            nc.vector.tensor_tensor(o[:], first_half[:, t0 : t0 + w], second_half[k][:], ADD)
             nc.sync.dma_start(out=out[:, t0 : t0 + w], in_=o[:])
 
-        for k in range(len(TAIL)):
-            fetch(k, 0)
-            if k > 0:
-                add(k - 1)
-            fetch(k, 1)
+        fetch(0)
+        for k in range(1, len(TAIL)):
+            fetch(k)
+            add(k - 1)
         add(len(TAIL) - 1)

from contextlib import ExitStack

import concourse.mybir as mybir
from concourse.masks import make_identity

K, T, E, C, H, N = 512, 1024, 16, 128, 512, 128
S = E * C
P = 128
FLOPS = 2 * K * H * S + 2 * H * N * S

F32 = mybir.dt.float32
BF16 = mybir.dt.bfloat16
I32 = mybir.dt.int32
U32 = mybir.dt.uint32
U16 = mybir.dt.uint16
U8 = mybir.dt.uint8
FP8X4 = mybir.dt.float8_e4m3fn_x4
FP4X4 = mybir.dt.float4_e2m1fn_x4
SILU = mybir.ActivationFunctionType.Silu
MULT = mybir.AluOpType.mult
ADD = mybir.AluOpType.add

X_CHUNKS = [256,256,256,256]
X_VECTOR = [160,160,160,160]
UNITS = [1,1,2,2,2,2,2,2,2]
GROUPS = [1,1,2,2,2,2,2,2,2]
T_ENG = "SSSSSSSSS"
Y_ENG = "VVVVVVVVV"
LT, LQ, LY, LEAD = 2, 3, 4, 2
PERM = "SQYGF"
TAIL = [512,384,128]


def tile_moe_pln_mlp_silu_kernel(
    tc, xT, w1_words, w1_scales, w2_words, w2_scales, gate, offs, pos1, pos2, out
):
    nc = tc.nc
    with ExitStack() as ctx:
        lists = ctx.enter_context(tc.tile_pool(name="lists", bufs=1))
        keep = ctx.enter_context(tc.tile_pool(name="keep", bufs=1))
        ring = ctx.enter_context(tc.tile_pool(name="ring", bufs=3))
        psum = ctx.enter_context(tc.psum_pool(name="psum", bufs=2))

        offs_sb = lists.tile([P, S // 16], U16, name="offs_sb")
        pos1_sb = lists.tile([P, T // 16], U16, name="pos1_sb")
        pos2_sb = lists.tile([P, T // 16], U16, name="pos2_sb")

        x_words = keep.tile([P, T], U32, name="x_words", align_bytes=64)
        x_scales = keep.tile([P, T], U8, name="x_scales", align_bytes=64)
        w1_sb = keep.tile([P, E, 2 * H], U8, name="w1_sb", align_bytes=64)
        w1s_sb = keep.tile([P, E, H], U8, name="w1s_sb", align_bytes=64)
        w2_sb = keep.tile([P, E, 2 * N], U8, name="w2_sb", align_bytes=64)
        w2s_sb = keep.tile([P, E, N], U8, name="w2s_sb", align_bytes=64)
        gate_sb = keep.tile([P, 2, T], F32, name="gate_sb")
        y_sb = keep.tile([P, S], F32, name="y_sb")
        ident = keep.tile([P, P], F32, name="ident")
        warm = keep.tile([P, 1], F32, name="warm")

        nc.sync.dma_start(offs_sb[:], offs)
        raws = []
        t0 = 0
        for c, w in enumerate(X_CHUNKS):
            raw = keep.tile([P, 4, w], F32, name=f"raw{c}")
            nc.sync.dma_start(out=raw[:], in_=xT[:, t0 : t0 + w].rearrange("(p j) w -> p j w", j=4))
            raws.append(raw)
            t0 += w

        nc.vector.memset(warm[:], 0.0)
        nc.scalar.activation(warm[:], warm[:], SILU)
        nc.gpsimd.memset(x_scales[:], 0)
        nc.vector.memset(w1s_sb[:].rearrange("p e i -> p (e i)").bitcast(I32), 0)
        nc.vector.memset(w2s_sb[:].rearrange("p e i -> p (e i)").bitcast(I32), 0)
        make_identity(nc, ident[:])

        def load_w1s(e0, e1):
            for q in range(4):
                nc.sync.dma_start(
                    out=w1s_sb[32 * q : 32 * q + 4, e0:e1, :].bitcast(I32),
                    in_=w1_scales[e0:e1, 0, 4 * q : 4 * q + 4, :].rearrange("e r i -> r e i").bitcast(I32),
                )

        def load_w2s(e0, e1):
            for q in range(4):
                nc.sync.dma_start(
                    out=w2s_sb[32 * q : 32 * q + 4, e0:e1, :].bitcast(I32),
                    in_=w2_scales[e0:e1, 0, 4 * q : 4 * q + 4, :].rearrange("e r i -> r e i").bitcast(I32),
                )

        def load_w1(e0, e1):
            nc.sync.dma_start(
                out=w1_sb[:, e0:e1, :].bitcast(I32),
                in_=w1_words[e0:e1, 0].rearrange("e p b -> p e b").bitcast(I32),
            )

        def load_w2(e0, e1):
            nc.sync.dma_start(
                out=w2_sb[:, e0:e1, :].bitcast(I32),
                in_=w2_words[e0:e1, 0].rearrange("e p b -> p e b").bitcast(I32),
            )

        load_w1s(0, 4)
        load_w1(0, 2)
        load_w1(2, 4)
        load_w1s(4, 16)
        load_w1(4, 8)
        load_w2s(0, 16)
        load_w2(0, 4)
        load_w1(8, 12)
        load_w2(4, 8)
        load_w1(12, 16)
        load_w2(8, 16)
        nc.sync.dma_start(pos1_sb[:], pos1)
        nc.sync.dma_start(pos2_sb[:], pos2)
        nc.sync.dma_start(out=gate_sb[:, 0, :], in_=gate[0])
        nc.sync.dma_start(out=gate_sb[:, 1, :], in_=gate[1])

        t0 = 0
        for c, w in enumerate(X_CHUNKS):
            grouped = ring.tile([P, w, 4], BF16, name="grouped", align_bytes=64)
            src = raws[c][:].rearrange("p j w -> p w j")
            v = X_VECTOR[c]
            if v > 0:
                nc.vector.tensor_copy(out=grouped[:, :v, :], in_=src[:, :v, :])
            if v < w:
                nc.scalar.copy(out=grouped[:, v:, :], in_=src[:, v:, :])
            nc.vector.quantize_mx(
                out=x_words[:, t0 : t0 + w].bitcast(FP8X4),
                scales=x_scales[:, t0 : t0 + w],
                in_=grouped[:].rearrange("p w j -> p (w j)"),
            )
            t0 += w

        starts = [sum(UNITS[:u]) for u in range(len(UNITS))]
        g_tiles, h_tiles, hg_tiles, q_tiles = {}, {}, {}, {}

        def gather(e0, e1):
            w = (e1 - e0) * C
            lst = offs_sb[:, e0 * C // 16 : e1 * C // 16]
            g_words = ring.tile([P, w], U32, name="g_words", bufs=3, align_bytes=64)
            g_scales = ring.tile([P, w], U8, name="g_scales", bufs=3, align_bytes=64)
            nc.vector.tensor_copy(out=g_words[:], in_=x_words[:].indirect(lst))
            nc.vector.tensor_copy(out=g_scales[:], in_=x_scales[:].indirect(lst))
            for e in range(e0, e1):
                slots = slice((e - e0) * C, (e - e0 + 1) * C)
                g_tiles[e] = g_words[:, slots], g_scales[:, slots]

        def first(u):
            h_tiles[u] = []
            for i in range(UNITS[u]):
                e = starts[u] + i
                words, scales = g_tiles[e]
                a_ps = psum.tile([P, H], F32, name="a_ps", bufs=4)
                nc.tensor.matmul_mx(
                    out=a_ps[:],
                    lhsT=words.bitcast(FP8X4),
                    lhsT_scale=scales,
                    rhs=w1_sb[:, e, :].bitcast(FP4X4),
                    rhs_scale=w1s_sb[:, e, :],
                    start=True,
                    stop=True,
                )
                h_sb = ring.tile([P, 2, P, 2], BF16, name="h_sb", bufs=8, align_bytes=64)
                nc.scalar.activation(h_sb[:], a_ps[:].rearrange("s (p u d) -> s u p d", u=2, d=2), SILU)
                h_tiles[u].append(h_sb)

        def turn(u):
            w = UNITS[u] * C
            t_ps = psum.tile([P, 2, w], F32, name="t_ps", bufs=2)
            for i in range(UNITS[u]):
                words = h_tiles[u][i][:].rearrange("s u p d -> s (u p d)").bitcast(F32)
                for v in range(2):
                    nc.tensor.transpose(t_ps[:, v, i * C : (i + 1) * C], words[:, v * P : (v + 1) * P], ident[:])
            hg = ring.tile([P, w, 4], BF16, name="hg", align_bytes=64)
            hg_words = hg[:].rearrange("p s j -> p (s j)").bitcast(F32).rearrange("p (s v) -> p s v", v=2)
            if T_ENG[u] == "V":
                nc.vector.tensor_copy(out=hg_words, in_=t_ps[:].rearrange("p v s -> p s v"))
            else:
                nc.scalar.copy(out=hg_words, in_=t_ps[:].rearrange("p v s -> p s v"))
            hg_tiles[u] = hg

        def quantize(u):
            w = UNITS[u] * C
            h_words = ring.tile([P, w], U32, name="h_words", align_bytes=64)
            h_scales = ring.tile([P, w], U8, name="h_scales", align_bytes=64)
            nc.vector.quantize_mx(
                out=h_words[:].bitcast(FP8X4), scales=h_scales[:], in_=hg_tiles[u][:].rearrange("p s j -> p (s j)")
            )
            q_tiles[u] = h_words, h_scales

        def second(u):
            w = UNITS[u] * C
            h_words, h_scales = q_tiles[u]
            y_ps = psum.tile([P, w], F32, name="y_ps", bufs=2)
            for i in range(UNITS[u]):
                e = starts[u] + i
                cols = slice(i * C, (i + 1) * C)
                nc.tensor.matmul_mx(
                    out=y_ps[:, cols],
                    lhsT=w2_sb[:, e, :].bitcast(FP4X4),
                    lhsT_scale=w2s_sb[:, e, :],
                    rhs=h_words[:, cols].bitcast(FP8X4),
                    rhs_scale=h_scales[:, cols],
                    start=True,
                    stop=True,
                )
            cols = slice(starts[u] * C, starts[u] * C + w)
            if Y_ENG[u] == "V":
                nc.vector.tensor_copy(out=y_sb[:, cols], in_=y_ps[:])
            else:
                nc.scalar.copy(out=y_sb[:, cols], in_=y_ps[:])

        n = len(UNITS)
        groups = list(GROUPS)
        have = 0
        for s in range(n + LY):
            for stage in PERM:
                if stage == "G":
                    last = min(n - 1, s + LEAD)
                    while have < starts[last] + UNITS[last]:
                        gather(have, have + groups[0])
                        have += groups.pop(0)
                if stage == "F" and s < n:
                    first(s)
                if stage == "S" and 0 <= s - LT < n:
                    turn(s - LT)
                if stage == "Q" and 0 <= s - LQ < n:
                    quantize(s - LQ)
                if stage == "Y" and 0 <= s - LY < n:
                    second(s - LY)

        first_half = keep.tile([P, T], F32, name="first_half")
        nc.vector.tensor_tensor(first_half[:], y_sb[:].indirect(pos1_sb[:]), gate_sb[:, 0, :], MULT)
        tail_starts = [sum(TAIL[:k]) for k in range(len(TAIL))]
        second_half = {}

        def fetch(k):
            t0, w = tail_starts[k], TAIL[k]
            half = ring.tile([P, w], F32, name=f"half_{k}", bufs=1)
            rows = slice(t0 // 16, (t0 + w) // 16)
            nc.vector.tensor_tensor(half[:], y_sb[:].indirect(pos2_sb[:, rows]), gate_sb[:, 1, t0 : t0 + w], MULT)
            second_half[k] = half

        def add(k):
            t0, w = tail_starts[k], TAIL[k]
            o = ring.tile([P, w], F32, name=f"o_{k}", bufs=1)
            nc.vector.tensor_tensor(o[:], first_half[:, t0 : t0 + w], second_half[k][:], ADD)
            nc.sync.dma_start(out=out[:, t0 : t0 + w], in_=o[:])

        fetch(0)
        for k in range(1, len(TAIL)):
            fetch(k)
            add(k - 1)
        add(len(TAIL) - 1)
